import numpy as np, ml_dtypes
CORES = [3,5,19,21,35,37,51,53,67,69]
N = 10
import mx_ref
NC, G, MB = 128, 2, 3
C = np.float32(0.019)
BF = ml_dtypes.bfloat16
def cut(t, i, w=512):
    return t[:, w * i:w * i + w]
def tile(rs):
    return np.stack(rs, axis=2).reshape(128, -1).astype(BF)
def layer(w, X):
    out = []
    for i in range(G):
        for t in range(len(X)):
            p = mx_ref.matmul(mx_ref.quantize(cut(w, len(X) * i + t)), X[t])
            z = p if t == 0 else z + p
        out.append(z)
    return out
def act(Z):
    return [np.maximum(s * z, 0) * C for z in Z for s in (1, -1)]
def setup_inputs(rng):
    def f(*shape):
        return mx_ref.flush((rng.standard_normal(shape, dtype=np.float32) * np.exp2(rng.integers(-2, 3, shape[:-1] + (1,)))).astype(BF))
    return {"x": f(N, 128, MB * 4 * NC), "w": f(N, 128, G * 512)}
def setup_inputs_blocks(rng):
    d = setup_inputs(rng)
    for k in ("x",): d[k] = mx_ref.spread(d[k], rng, 4)
    for k in ("w",): d[k] = mx_ref.spread(d[k], rng, 1)
    return d
def setup_inputs_wide(rng):
    d = setup_inputs(rng)
    for k in ("x",): d[k] = mx_ref.flush((d[k].astype(np.float32) * np.exp2(rng.integers(-8, 9, (N, 1, 1))).astype(np.float32)).astype(BF))
    return d
def setup_inputs_zeros(rng):
    d = setup_inputs(rng); v = d["x"].reshape(N, 128, -1, 4).copy()
    v[np.broadcast_to((rng.random((N, 1, v.shape[2], 1)) < 0.33), v.shape)] = 0
    d["x"] = v.reshape(d["x"].shape)
    return d
def reference(x, w):
    y = np.full((N, 128, MB * G * NC), np.nan, np.float32)
    for m in range(MB):
        a = mx_ref.quantize(cut(x[N - 1], m, 4 * NC))
        for s in range(N - 1):
            a = mx_ref.quantize(tile(act(layer(w[s], [a]))))
        Z = layer(w[N - 1], [a])
        for i in range(G):
            y[N - 1][:, NC * (G * m + i):NC * (G * m + i) + NC] = Z[i]
    return {"y": y}

@@ -1,0 +1,107 @@
+from concourse.mybir import dt, AluOpType, ActivationFunctionType
+
+N, MB, G, NC = 10, 3, 2, 128
+C = 0.019
+TW = 4 * NC
+
+K_ON = (8, 8, 8)
+K_OFF = (8, 8, 8)
+
+SCRATCH = {
+    "wt": ("sbuf", [128, G * TW], "bfloat16"),
+    "wq": ("sbuf", [128, G * NC], "float8_e4m3fn_x4"),
+    "wp": ("sbuf", [128, G * NC], "uint8"),
+    "ps": ("psum", [128, 512 * G * MB], "float32"),
+    "ysb": ("sbuf", [128, G * MB * NC], "float32"),
+}
+SEMAPHORES = ["lw", "wqd", "sent", "st"]
+for _m in range(MB):
+    SCRATCH["xt%d" % _m] = ("sbuf", [128, TW], "bfloat16")
+    SCRATCH["h%d" % _m] = ("sbuf", [128, TW], "bfloat16")
+    SCRATCH["oq%d" % _m] = ("sbuf", [128, NC], "float8_e4m3fn_x4")
+    SCRATCH["op%d" % _m] = ("sbuf", [128, NC], "uint8")
+    SCRATCH["aq%d" % _m] = ("sbuf", [128, NC], "float8_e4m3fn_x4")
+    SCRATCH["ap%d" % _m] = ("sbuf", [128, NC], "uint8")
+    SEMAPHORES += ["lx%d" % _m, "arr%d" % _m, "hd%d" % _m, "qd%d" % _m]
+    SEMAPHORES += ["z%d%d" % (_m, _i) for _i in range(G)] + ["c%d%d" % (_m, _i) for _i in range(G)]
+
+
+def _engines(topo, src, dst, m):
+    allowed = topo.mask(src, dst)
+    bits = [b for b in range(allowed.bit_length()) if (allowed >> b) & 1]
+    k = min((K_ON if topo.chip(src) == topo.chip(dst) else K_OFF)[m], len(bits))
+    mask = 0
+    for b in bits[::len(bits) // k][:k]:
+        mask |= 1 << b
+    return mask, k
+
+
+def rank_program(g, core, T, topo):
+    rank = T.rank_of(core)
+    if rank is None:
+        return
+    last = rank == N - 1
+    nxt, prev = T.cores[(rank + 1) % N], T.cores[(rank - 1) % N]
+    assert topo.may_write(core, nxt)
+    rid, pid, _ = topo.addr(nxt)
+    S, V, A, PE, SY = T.sem, g.vector, g.scalar, g.tensor, g.sync
+
+    def bank(m, i):
+        b = 512 * (G * m + i)
+        return T.ps[:, b:b + NC]
+
+    if last:
+        SY.dma_start(T.xt0[:], T.x[:, 0:TW]).then_inc(S.lx0, 16)
+        A.dma_start(T.xt1[:], T.x[:, TW:2 * TW]).then_inc(S.lx1, 16)
+        SY.dma_start(T.xt2[:], T.x[:, 2 * TW:3 * TW]).then_inc(S.lx2, 16)
+        A.dma_start(T.wt[:], T.w[:]).then_inc(S.lw, 16)
+        for m in range(MB):
+            V.wait_ge(S["lx%d" % m], 16)
+            V.quantize_mx(T["oq%d" % m][:], T["op%d" % m][:], T["xt%d" % m][:]).then_inc(S["qd%d" % m], 1)
+    else:
+        SY.dma_start(T.wt[:], T.w[:]).then_inc(S.lw, 16)
+    V.wait_ge(S.lw, 16)
+    V.quantize_mx(T.wq[:], T.wp[:], T.wt[:]).then_inc(S.wqd, 1)
+
+    PE.wait_ge(S.wqd, 1)
+    for m in range(MB):
+        PE.wait_ge(S["arr%d" % m], 2 * _engines(topo, prev, core, m)[1])
+        for i in range(G):
+            PE.matmul_mx(bank(m, i), T.wq[:, NC * i:NC * i + NC], T.wp[:, NC * i:NC * i + NC],
+                         T["aq%d" % m][:], T["ap%d" % m][:], True, True).then_inc(S["z%d%d" % (m, i)], 1)
+
+    for m in range(MB):
+        z0, z1 = S["z%d0" % m], S["z%d1" % m]
+        if last:
+            c0, c1 = S["c%d0" % m], S["c%d1" % m]
+            a, b = NC * G * m, NC * (G * m + 1)
+            A.wait_ge(z0, 1)
+            A.activation(T.ysb[:, a:a + NC], bank(m, 0), ActivationFunctionType.Copy).then_inc(c0, 1)
+            A.wait_ge(c0, 1)
+            A.dma_start(T.y[:, a:a + NC], T.ysb[:, a:a + NC]).then_inc(S.st, 16)
+            V.wait_ge(z1, 1)
+            V.tensor_copy(T.ysb[:, b:b + NC], bank(m, 1)).then_inc(c1, 1)
+            SY.wait_ge(c1, 1)
+            SY.dma_start(T.y[:, b:b + NC], T.ysb[:, b:b + NC]).then_inc(S.st, 16)
+        else:
+            h, hd = T["h%d" % m], S["hd%d" % m]
+            A.wait_ge(z0, 1)
+            A.activation(h[:, 0:TW:4], bank(m, 0), ActivationFunctionType.Relu, scale=C).then_inc(hd, 1)
+            A.activation(h[:, 1:TW:4], bank(m, 0), ActivationFunctionType.Relu, scale=-C).then_inc(hd, 1)
+            V.wait_ge(z1, 1)
+            V.tensor_scalar(h[:, 2:TW:4], bank(m, 1), 0.0, C, AluOpType.max, AluOpType.mult).then_inc(hd, 1)
+            V.tensor_scalar(h[:, 3:TW:4], bank(m, 1), -C, 0.0, AluOpType.mult, AluOpType.max).then_inc(hd, 1)
+            V.wait_ge(hd, 4)
+            V.quantize_mx(T["oq%d" % m][:], T["op%d" % m][:], h[:]).then_inc(S["qd%d" % m], 1)
+
+    total = 0
+    for m in range(MB):
+        mask, k = _engines(topo, core, nxt, m)
+        g.wait_ge(S["qd%d" % m], 1)
+        g.remote_dma(T["aq%d" % m][:].bitcast(dt.uint8), T["oq%d" % m][:].bitcast(dt.uint8),
+                     S["arr%d" % m], S.sent, pid, rid, mask)
+        g.remote_dma(T["ap%d" % m][:], T["op%d" % m][:], S["arr%d" % m], S.sent, pid, rid, mask)
+        total += 2 * k
+    g.wait_ge(S.sent, total)
+    if last:
+        g.wait_ge(S.st, 16 * G * MB)

@@ -2,106 +2,155 @@ from concourse.mybir import dt, AluOpType, ActivationFunctionType
 
 N, MB, G, NC = 10, 3, 2, 128
 C = 0.019
-TW = 4 * NC
-
-K_ON = (8, 8, 8)
-K_OFF = (8, 8, 8)
+NG = 2
+GW = MB * NC // NG
+TW = 4 * GW
+PAIRED = N - 2
 
 SCRATCH = {
-    "wt": ("sbuf", [128, G * TW], "bfloat16"),
+    "wt": ("sbuf", [128, G * 4 * NC], "bfloat16"),
     "wq": ("sbuf", [128, G * NC], "float8_e4m3fn_x4"),
     "wp": ("sbuf", [128, G * NC], "uint8"),
-    "ps": ("psum", [128, 512 * G * MB], "float32"),
-    "ysb": ("sbuf", [128, G * MB * NC], "float32"),
+    "fq": ("sbuf", [128, G * NC], "float8_e4m3fn_x4"),
+    "fp": ("sbuf", [128, G * NC], "uint8"),
+    "ps": ("psum", [128, 512 * G * NG], "float32"),
+    "ysb": ("sbuf", [128, G * NG * GW], "float32"),
 }
-SEMAPHORES = ["lw", "wqd", "sent", "st"]
-for _m in range(MB):
-    SCRATCH["xt%d" % _m] = ("sbuf", [128, TW], "bfloat16")
-    SCRATCH["h%d" % _m] = ("sbuf", [128, TW], "bfloat16")
-    SCRATCH["oq%d" % _m] = ("sbuf", [128, NC], "float8_e4m3fn_x4")
-    SCRATCH["op%d" % _m] = ("sbuf", [128, NC], "uint8")
-    SCRATCH["aq%d" % _m] = ("sbuf", [128, NC], "float8_e4m3fn_x4")
-    SCRATCH["ap%d" % _m] = ("sbuf", [128, NC], "uint8")
-    SEMAPHORES += ["lx%d" % _m, "arr%d" % _m, "hd%d" % _m, "qd%d" % _m]
-    SEMAPHORES += ["z%d%d" % (_m, _i) for _i in range(G)] + ["c%d%d" % (_m, _i) for _i in range(G)]
+SEMAPHORES = ["lw", "wqd", "warr", "sent", "st"]
+for _k in range(NG):
+    SCRATCH["xt%d" % _k] = ("sbuf", [128, TW], "bfloat16")
+    SCRATCH["h%d" % _k] = ("sbuf", [128, TW], "bfloat16")
+    SCRATCH["oq%d" % _k] = ("sbuf", [128, GW], "float8_e4m3fn_x4")
+    SCRATCH["op%d" % _k] = ("sbuf", [128, GW], "uint8")
+    SCRATCH["aq%d" % _k] = ("sbuf", [128, GW], "float8_e4m3fn_x4")
+    SCRATCH["ap%d" % _k] = ("sbuf", [128, GW], "uint8")
+    SEMAPHORES += ["lx%d" % _k, "arr%d" % _k, "hd%d" % _k, "qd%d" % _k]
+    SEMAPHORES += ["z%d%d" % (_k, _i) for _i in range(G)] + ["c%d%d" % (_k, _i) for _i in range(G)]
 
 
-def _engines(topo, src, dst, m):
+def _engines(topo, src, dst, share=1, part=0):
     allowed = topo.mask(src, dst)
-    bits = [b for b in range(allowed.bit_length()) if (allowed >> b) & 1]
-    k = min((K_ON if topo.chip(src) == topo.chip(dst) else K_OFF)[m], len(bits))
+    bits = [b for b in range(allowed.bit_length()) if (allowed >> b) & 1][part::share]
     mask = 0
-    for b in bits[::len(bits) // k][:k]:
+    for b in bits:
         mask |= 1 << b
-    return mask, k
+    return mask, len(bits)
+
+
+def _sends(r):
+    if r == N - 1:
+        return [(q, q, 0, 1, 0) for q in range(NG)]
+    if r == N - 2:
+        return [(q, N - 1, q, NG, q) for q in range(NG)]
+    return [(1, r + NG, 0, 1, 0)] if r + NG < PAIRED else [(1, N - 2, r % NG, 1, 0)]
+
+
+def _pieces(q, i):
+    out, j = [], 0
+    while j < GW:
+        m, o = divmod(GW * q + j, NC)
+        w = min(NC - o, GW - j)
+        out.append((j, NC * (G * m + i) + o, w))
+        j += w
+    return out
 
 
 def rank_program(g, core, T, topo):
     rank = T.rank_of(core)
     if rank is None:
         return
-    last = rank == N - 1
-    nxt, prev = T.cores[(rank + 1) % N], T.cores[(rank - 1) % N]
-    assert topo.may_write(core, nxt)
-    rid, pid, _ = topo.addr(nxt)
+    last, paired = rank == N - 1, rank < PAIRED
     S, V, A, PE, SY = T.sem, g.vector, g.scalar, g.tensor, g.sync
+    u8 = dt.uint8
 
-    def bank(m, i):
-        b = 512 * (G * m + i)
-        return T.ps[:, b:b + NC]
+    def bank(k, i):
+        b = 512 * (G * k + i)
+        return T.ps[:, b:b + GW]
+
+    arrive = {}
+    for r in range(N):
+        for _, d, slot, share, part in _sends(r):
+            if d == rank:
+                arrive[slot] = 2 * _engines(topo, T.cores[r], core, share, part)[1]
 
     if last:
         SY.dma_start(T.xt0[:], T.x[:, 0:TW]).then_inc(S.lx0, 16)
         A.dma_start(T.xt1[:], T.x[:, TW:2 * TW]).then_inc(S.lx1, 16)
-        SY.dma_start(T.xt2[:], T.x[:, 2 * TW:3 * TW]).then_inc(S.lx2, 16)
-        A.dma_start(T.wt[:], T.w[:]).then_inc(S.lw, 16)
-        for m in range(MB):
-            V.wait_ge(S["lx%d" % m], 16)
-            V.quantize_mx(T["oq%d" % m][:], T["op%d" % m][:], T["xt%d" % m][:]).then_inc(S["qd%d" % m], 1)
+        SY.dma_start(T.wt[:], T.w[:]).then_inc(S.lw, 16)
+        for q in range(NG):
+            V.wait_ge(S["lx%d" % q], 16)
+            V.quantize_mx(T["oq%d" % q][:], T["op%d" % q][:], T["xt%d" % q][:]).then_inc(S["qd%d" % q], 1)
     else:
         SY.dma_start(T.wt[:], T.w[:]).then_inc(S.lw, 16)
     V.wait_ge(S.lw, 16)
     V.quantize_mx(T.wq[:], T.wp[:], T.wt[:]).then_inc(S.wqd, 1)
 
-    PE.wait_ge(S.wqd, 1)
-    for m in range(MB):
-        PE.wait_ge(S["arr%d" % m], 2 * _engines(topo, prev, core, m)[1])
-        for i in range(G):
-            PE.matmul_mx(bank(m, i), T.wq[:, NC * i:NC * i + NC], T.wp[:, NC * i:NC * i + NC],
-                         T["aq%d" % m][:], T["ap%d" % m][:], True, True).then_inc(S["z%d%d" % (m, i)], 1)
-
-    for m in range(MB):
-        z0, z1 = S["z%d0" % m], S["z%d1" % m]
-        if last:
-            c0, c1 = S["c%d0" % m], S["c%d1" % m]
-            a, b = NC * G * m, NC * (G * m + 1)
-            A.wait_ge(z0, 1)
-            A.activation(T.ysb[:, a:a + NC], bank(m, 0), ActivationFunctionType.Copy).then_inc(c0, 1)
-            A.wait_ge(c0, 1)
-            A.dma_start(T.y[:, a:a + NC], T.ysb[:, a:a + NC]).then_inc(S.st, 16)
-            V.wait_ge(z1, 1)
-            V.tensor_copy(T.ysb[:, b:b + NC], bank(m, 1)).then_inc(c1, 1)
-            SY.wait_ge(c1, 1)
-            SY.dma_start(T.y[:, b:b + NC], T.ysb[:, b:b + NC]).then_inc(S.st, 16)
+    if paired:
+        mate = T.cores[rank + 1 if rank % NG == 0 else rank - 1]
+        wmask, wk = _engines(topo, core, mate)
+        wk_in = _engines(topo, mate, core)[1]
+    for k in range(NG):
+        own = not paired or rank % NG == k
+        wq, wp = (T.wq, T.wp) if own else (T.fq, T.fp)
+        if own:
+            PE.wait_ge(S.wqd, 1)
         else:
-            h, hd = T["h%d" % m], S["hd%d" % m]
+            PE.wait_ge(S.warr, 2 * wk_in)
+        if paired and k == 1:
+            mq, mp = T.oq0, T.op0
+            PE.wait_ge(S.qd0, 1)
+        else:
+            mq, mp = T["aq%d" % k], T["ap%d" % k]
+            PE.wait_ge(S["arr%d" % k], arrive[k])
+        for i in range(G):
+            PE.matmul_mx(bank(k, i), wq[:, NC * i:NC * i + NC], wp[:, NC * i:NC * i + NC],
+                         mq[:], mp[:], True, True).then_inc(S["z%d%d" % (k, i)], 1)
+
+    stores = 0
+    for k in range(NG):
+        z0, z1 = S["z%d0" % k], S["z%d1" % k]
+        if last:
+            c0, c1 = S["c%d0" % k], S["c%d1" % k]
+            a, b = GW * G * k, GW * (G * k + 1)
             A.wait_ge(z0, 1)
-            A.activation(h[:, 0:TW:4], bank(m, 0), ActivationFunctionType.Relu, scale=C).then_inc(hd, 1)
-            A.activation(h[:, 1:TW:4], bank(m, 0), ActivationFunctionType.Relu, scale=-C).then_inc(hd, 1)
+            A.activation(T.ysb[:, a:a + GW], bank(k, 0), ActivationFunctionType.Copy).then_inc(c0, 1)
             V.wait_ge(z1, 1)
-            V.tensor_scalar(h[:, 2:TW:4], bank(m, 1), 0.0, C, AluOpType.max, AluOpType.mult).then_inc(hd, 1)
-            V.tensor_scalar(h[:, 3:TW:4], bank(m, 1), -C, 0.0, AluOpType.mult, AluOpType.max).then_inc(hd, 1)
+            V.tensor_copy(T.ysb[:, b:b + GW], bank(k, 1)).then_inc(c1, 1)
+            A.wait_ge(c0, 1)
+            for j, yc, w in _pieces(k, 0):
+                A.dma_start(T.y[:, yc:yc + w], T.ysb[:, a + j:a + j + w]).then_inc(S.st, 16)
+            SY.wait_ge(c1, 1)
+            A.wait_ge(c1, 1)
+            for j, yc, w in _pieces(k, 1):
+                (SY if w == NC else A).dma_start(T.y[:, yc:yc + w], T.ysb[:, b + j:b + j + w]).then_inc(S.st, 16)
+            stores += len(_pieces(k, 0)) + len(_pieces(k, 1))
+        else:
+            h, hd = T["h%d" % k], S["hd%d" % k]
+            A.wait_ge(z0, 1)
+            A.activation(h[:, 0:TW:4], bank(k, 0), ActivationFunctionType.Relu, scale=C).then_inc(hd, 1)
+            A.activation(h[:, 1:TW:4], bank(k, 0), ActivationFunctionType.Relu, scale=-C).then_inc(hd, 1)
+            V.wait_ge(z1, 1)
+            V.tensor_scalar(h[:, 2:TW:4], bank(k, 1), 0.0, C, AluOpType.max, AluOpType.mult).then_inc(hd, 1)
+            V.tensor_scalar(h[:, 3:TW:4], bank(k, 1), -C, 0.0, AluOpType.mult, AluOpType.max).then_inc(hd, 1)
             V.wait_ge(hd, 4)
-            V.quantize_mx(T["oq%d" % m][:], T["op%d" % m][:], h[:]).then_inc(S["qd%d" % m], 1)
+            V.quantize_mx(T["oq%d" % k][:], T["op%d" % k][:], h[:]).then_inc(S["qd%d" % k], 1)
 
     total = 0
-    for m in range(MB):
-        mask, k = _engines(topo, core, nxt, m)
-        g.wait_ge(S["qd%d" % m], 1)
-        g.remote_dma(T["aq%d" % m][:].bitcast(dt.uint8), T["oq%d" % m][:].bitcast(dt.uint8),
-                     S["arr%d" % m], S.sent, pid, rid, mask)
-        g.remote_dma(T["ap%d" % m][:], T["op%d" % m][:], S["arr%d" % m], S.sent, pid, rid, mask)
-        total += 2 * k
+    if paired:
+        rid, pid, _ = topo.addr(mate)
+        g.wait_ge(S.wqd, 1)
+        g.remote_dma(T.fq[:].bitcast(u8), T.wq[:].bitcast(u8), S.warr, S.sent, pid, rid, wmask)
+        g.remote_dma(T.fp[:], T.wp[:], S.warr, S.sent, pid, rid, wmask)
+        total += 2 * wk
+    for k, d, slot, share, part in _sends(rank):
+        dst = T.cores[d]
+        assert topo.may_write(core, dst)
+        rid, pid, _ = topo.addr(dst)
+        mask, n = _engines(topo, core, dst, share, part)
+        g.wait_ge(S["qd%d" % k], 1)
+        g.remote_dma(T["aq%d" % slot][:].bitcast(u8), T["oq%d" % k][:].bitcast(u8), S["arr%d" % slot], S.sent, pid, rid, mask)
+        g.remote_dma(T["ap%d" % slot][:], T["op%d" % k][:], S["arr%d" % slot], S.sent, pid, rid, mask)
+        total += 2 * n
     g.wait_ge(S.sent, total)
     if last:
-        g.wait_ge(S.st, 16 * G * MB)
+        g.wait_ge(S.st, 16 * stores)

@@ -5,44 +5,106 @@ C = 0.019
 NG = 2
 GW = MB * NC // NG
 TW = 4 * GW
-PAIRED = N - 2
+WW = G * NC
+SINGLE = 0
+PAIRS = [(r, r + 1) for r in range(1, N - 1, 2)]
 
 SCRATCH = {
     "wt": ("sbuf", [128, G * 4 * NC], "bfloat16"),
-    "wq": ("sbuf", [128, G * NC], "float8_e4m3fn_x4"),
-    "wp": ("sbuf", [128, G * NC], "uint8"),
-    "fq": ("sbuf", [128, G * NC], "float8_e4m3fn_x4"),
-    "fp": ("sbuf", [128, G * NC], "uint8"),
+    "wq": ("sbuf", [128, WW], "float8_e4m3fn_x4"),
+    "wp": ("sbuf", [128, WW], "uint8"),
+    "fq": ("sbuf", [128, WW], "float8_e4m3fn_x4"),
+    "fp": ("sbuf", [128, WW], "uint8"),
+    "rp": ("sbuf", [128, WW], "uint8"),
+    "op": ("sbuf", [128, NG * GW], "uint8"),
+    "ap": ("sbuf", [128, NG * GW], "uint8"),
     "ps": ("psum", [128, 512 * G * NG], "float32"),
     "ysb": ("sbuf", [128, G * NG * GW], "float32"),
 }
-SEMAPHORES = ["lw", "wqd", "warr", "sent", "st"]
+SEMAPHORES = ["lw", "wqd", "warr", "rarr", "sent", "st"]
 for _k in range(NG):
     SCRATCH["xt%d" % _k] = ("sbuf", [128, TW], "bfloat16")
     SCRATCH["h%d" % _k] = ("sbuf", [128, TW], "bfloat16")
     SCRATCH["oq%d" % _k] = ("sbuf", [128, GW], "float8_e4m3fn_x4")
-    SCRATCH["op%d" % _k] = ("sbuf", [128, GW], "uint8")
     SCRATCH["aq%d" % _k] = ("sbuf", [128, GW], "float8_e4m3fn_x4")
-    SCRATCH["ap%d" % _k] = ("sbuf", [128, GW], "uint8")
     SEMAPHORES += ["lx%d" % _k, "arr%d" % _k, "hd%d" % _k, "qd%d" % _k]
     SEMAPHORES += ["z%d%d" % (_k, _i) for _i in range(G)] + ["c%d%d" % (_k, _i) for _i in range(G)]
 
 
-def _engines(topo, src, dst, share=1, part=0):
-    allowed = topo.mask(src, dst)
-    bits = [b for b in range(allowed.bit_length()) if (allowed >> b) & 1][part::share]
-    mask = 0
-    for b in bits:
-        mask |= 1 << b
-    return mask, len(bits)
+def _count(mask):
+    return bin(mask).count("1")
 
 
-def _sends(r):
-    if r == N - 1:
-        return [(q, q, 0, 1, 0) for q in range(NG)]
-    if r == N - 2:
-        return [(q, N - 1, q, NG, q) for q in range(NG)]
-    return [(1, r + NG, 0, 1, 0)] if r + NG < PAIRED else [(1, N - 2, r % NG, 1, 0)]
+def _layout(T, topo):
+    cores = T.cores
+
+    def chip(r):
+        return topo.chip(cores[r])
+
+    def mask(a, b):
+        return topo.mask(cores[a], cores[b])
+
+    ways = [[SINGLE], [SINGLE]]
+    for a, b in PAIRS:
+        keep = int(chip(ways[0][-1]) == chip(a)) + int(chip(ways[1][-1]) == chip(b))
+        turn = int(chip(ways[0][-1]) == chip(b)) + int(chip(ways[1][-1]) == chip(a))
+        u, v = (a, b) if keep >= turn else (b, a)
+        ways[0].append(u)
+        ways[1].append(v)
+    for w in ways:
+        w.append(N - 1)
+    ways.sort(key=lambda w: sum(int(chip(w[j]) == chip(w[j + 1])) for j in range(len(w) - 1)))
+
+    near = None
+    for a, b in PAIRS:
+        for u in (a, b):
+            if chip(u) == chip(SINGLE):
+                near = u
+
+    out = []
+
+    def tile(src, k, dst, slot, m):
+        out.append((src, "qd%d" % k, dst, ("aq%d" % slot, 0, GW), ("oq%d" % k, 0, GW), True, "arr%d" % slot, m))
+        out.append((src, None, dst, ("ap", GW * slot, GW * slot + GW), ("op", GW * k, GW * k + GW), False, "arr%d" % slot, m))
+
+    m = mask(N - 1, SINGLE)
+    out.append((N - 1, "qd0", SINGLE, ("aq0", 0, GW), ("oq0", 0, GW), True, "arr0", m))
+    out.append((N - 1, "qd1", SINGLE, ("ap", 0, NG * GW), ("op", 0, NG * GW), False, "arr0", m))
+    out.append((N - 1, None, SINGLE, ("aq1", 0, GW), ("oq1", 0, GW), True, "arr1", m))
+
+    hop = {}
+    for w in ways:
+        for j in range(1, len(w) - 1):
+            hop[w[j]] = w[j + 1]
+    passed = []
+    for a, b in PAIRS:
+        for u, v in ((a, b), (b, a)):
+            m = mask(u, v)
+            via = [SINGLE if v == near else None, hop[u] if chip(hop[u]) == chip(u) else None]
+            seq = []
+            for i in range(G):
+                if via[i] is not None:
+                    lo, hi = NC * i, NC * i + NC
+                    seq.append((via[i], ("rp", lo, hi), ("wp", lo, hi), False, "rarr", mask(u, via[i])))
+                    passed.append((via[i], "rarr", v, ("fp", lo, hi), ("rp", lo, hi), False, "warr", mask(via[i], v)))
+            seq.append((v, ("fq", 0, WW), ("wq", 0, WW), True, "warr", m))
+            if via == [None] * G:
+                seq.append((v, ("fp", 0, WW), ("wp", 0, WW), False, "warr", m))
+            else:
+                for i in range(G):
+                    if via[i] is None:
+                        seq.append((v, ("fp", NC * i, NC * i + NC), ("wp", NC * i, NC * i + NC), False, "warr", m))
+            for n, t in enumerate(seq):
+                out.append((u, "wqd" if n == 0 else None) + t)
+    out += passed
+
+    for q, w in enumerate(ways):
+        m = mask(SINGLE, w[1])
+        spare = m & ~mask(SINGLE, ways[1 - q][1])
+        tile(SINGLE, q, w[1], 0, spare if spare else m)
+        for j in range(1, len(w) - 1):
+            tile(w[j], 1, w[j + 1], q if w[j + 1] == N - 1 else 0, mask(w[j], w[j + 1]))
+    return out
 
 
 def _pieces(q, i):
@@ -59,71 +121,63 @@ def rank_program(g, core, T, topo):
     rank = T.rank_of(core)
     if rank is None:
         return
-    last, paired = rank == N - 1, rank < PAIRED
+    last = rank == N - 1
+    pair = None
+    for p in PAIRS:
+        if rank in p:
+            pair = p
+    paired = pair is not None
     S, V, A, PE, SY = T.sem, g.vector, g.scalar, g.tensor, g.sync
     u8 = dt.uint8
 
-    def bank(k, i):
+    def bank(k, i, lo=0, hi=GW):
         b = 512 * (G * k + i)
-        return T.ps[:, b:b + GW]
+        return T.ps[:, b + lo:b + hi]
 
+    writes = _layout(T, topo)
     arrive = {}
-    for r in range(N):
-        for _, d, slot, share, part in _sends(r):
-            if d == rank:
-                arrive[slot] = 2 * _engines(topo, T.cores[r], core, share, part)[1]
+    for _, _, dst, _, _, _, sem, m in writes:
+        if dst == rank:
+            arrive[sem] = arrive.get(sem, 0) + _count(m)
 
     if last:
         SY.dma_start(T.xt0[:], T.x[:, 0:TW]).then_inc(S.lx0, 16)
-        A.dma_start(T.xt1[:], T.x[:, TW:2 * TW]).then_inc(S.lx1, 16)
+        SY.dma_start(T.xt1[:], T.x[:, TW:2 * TW]).then_inc(S.lx1, 16)
         SY.dma_start(T.wt[:], T.w[:]).then_inc(S.lw, 16)
         for q in range(NG):
             V.wait_ge(S["lx%d" % q], 16)
-            V.quantize_mx(T["oq%d" % q][:], T["op%d" % q][:], T["xt%d" % q][:]).then_inc(S["qd%d" % q], 1)
+            V.quantize_mx(T["oq%d" % q][:], T.op[:, GW * q:GW * q + GW], T["xt%d" % q][:]).then_inc(S["qd%d" % q], 1)
     else:
         SY.dma_start(T.wt[:], T.w[:]).then_inc(S.lw, 16)
     V.wait_ge(S.lw, 16)
     V.quantize_mx(T.wq[:], T.wp[:], T.wt[:]).then_inc(S.wqd, 1)
 
-    if paired:
-        mate = T.cores[rank + 1 if rank % NG == 0 else rank - 1]
-        wmask, wk = _engines(topo, core, mate)
-        wk_in = _engines(topo, mate, core)[1]
     for k in range(NG):
-        own = not paired or rank % NG == k
+        own = not paired or pair[k] == rank
         wq, wp = (T.wq, T.wp) if own else (T.fq, T.fp)
         if own:
             PE.wait_ge(S.wqd, 1)
         else:
-            PE.wait_ge(S.warr, 2 * wk_in)
+            PE.wait_ge(S.warr, arrive["warr"])
         if paired and k == 1:
-            mq, mp = T.oq0, T.op0
+            mq, mp = T.oq0[:], T.op[:, 0:GW]
             PE.wait_ge(S.qd0, 1)
         else:
-            mq, mp = T["aq%d" % k], T["ap%d" % k]
-            PE.wait_ge(S["arr%d" % k], arrive[k])
+            mq, mp = T["aq%d" % k][:], T.ap[:, GW * k:GW * k + GW]
+            PE.wait_ge(S["arr%d" % k], arrive["arr%d" % k])
         for i in range(G):
             PE.matmul_mx(bank(k, i), wq[:, NC * i:NC * i + NC], wp[:, NC * i:NC * i + NC],
-                         mq[:], mp[:], True, True).then_inc(S["z%d%d" % (k, i)], 1)
+                         mq, mp, True, True).then_inc(S["z%d%d" % (k, i)], 1)
 
-    stores = 0
     for k in range(NG):
         z0, z1 = S["z%d0" % k], S["z%d1" % k]
         if last:
-            c0, c1 = S["c%d0" % k], S["c%d1" % k]
-            a, b = GW * G * k, GW * (G * k + 1)
             A.wait_ge(z0, 1)
-            A.activation(T.ysb[:, a:a + GW], bank(k, 0), ActivationFunctionType.Copy).then_inc(c0, 1)
-            V.wait_ge(z1, 1)
-            V.tensor_copy(T.ysb[:, b:b + GW], bank(k, 1)).then_inc(c1, 1)
-            A.wait_ge(c0, 1)
             for j, yc, w in _pieces(k, 0):
-                A.dma_start(T.y[:, yc:yc + w], T.ysb[:, a + j:a + j + w]).then_inc(S.st, 16)
-            SY.wait_ge(c1, 1)
-            A.wait_ge(c1, 1)
+                A.activation(T.ysb[:, yc:yc + w], bank(k, 0, j, j + w), ActivationFunctionType.Copy).then_inc(S["c%d0" % k], 1)
+            V.wait_ge(z1, 1)
             for j, yc, w in _pieces(k, 1):
-                (SY if w == NC else A).dma_start(T.y[:, yc:yc + w], T.ysb[:, b + j:b + j + w]).then_inc(S.st, 16)
-            stores += len(_pieces(k, 0)) + len(_pieces(k, 1))
+                V.tensor_copy(T.ysb[:, yc:yc + w], bank(k, 1, j, j + w)).then_inc(S["c%d1" % k], 1)
         else:
             h, hd = T["h%d" % k], S["hd%d" % k]
             A.wait_ge(z0, 1)
@@ -133,24 +187,36 @@ def rank_program(g, core, T, topo):
             V.tensor_scalar(h[:, 2:TW:4], bank(k, 1), 0.0, C, AluOpType.max, AluOpType.mult).then_inc(hd, 1)
             V.tensor_scalar(h[:, 3:TW:4], bank(k, 1), -C, 0.0, AluOpType.mult, AluOpType.max).then_inc(hd, 1)
             V.wait_ge(hd, 4)
-            V.quantize_mx(T["oq%d" % k][:], T["op%d" % k][:], h[:]).then_inc(S["qd%d" % k], 1)
+            V.quantize_mx(T["oq%d" % k][:], T.op[:, GW * k:GW * k + GW], h[:]).then_inc(S["qd%d" % k], 1)
+    if last:
+        cut, grown = 0, True
+        while grown:
+            grown = False
+            for i in range(G):
+                for _, yc, w in _pieces(0, i):
+                    if yc == cut:
+                        cut, grown = cut + w, True
+        for i in range(G):
+            SY.wait_ge(S["c0%d" % i], len(_pieces(0, i)))
+        SY.dma_start(T.y[:, 0:cut], T.ysb[:, 0:cut]).then_inc(S.st, 16)
+        for i in range(G):
+            SY.wait_ge(S["c1%d" % i], len(_pieces(1, i)))
+        SY.dma_start(T.y[:, cut:], T.ysb[:, cut:]).then_inc(S.st, 16)
 
     total = 0
-    if paired:
-        rid, pid, _ = topo.addr(mate)
-        g.wait_ge(S.wqd, 1)
-        g.remote_dma(T.fq[:].bitcast(u8), T.wq[:].bitcast(u8), S.warr, S.sent, pid, rid, wmask)
-        g.remote_dma(T.fp[:], T.wp[:], S.warr, S.sent, pid, rid, wmask)
-        total += 2 * wk
-    for k, d, slot, share, part in _sends(rank):
-        dst = T.cores[d]
-        assert topo.may_write(core, dst)
-        rid, pid, _ = topo.addr(dst)
-        mask, n = _engines(topo, core, dst, share, part)
-        g.wait_ge(S["qd%d" % k], 1)
-        g.remote_dma(T["aq%d" % slot][:].bitcast(u8), T["oq%d" % k][:].bitcast(u8), S["arr%d" % slot], S.sent, pid, rid, mask)
-        g.remote_dma(T["ap%d" % slot][:], T["op%d" % k][:], S["arr%d" % slot], S.sent, pid, rid, mask)
-        total += 2 * n
+    for src, wait, dst, o, i, codes, sem, m in writes:
+        if src != rank:
+            continue
+        d = T.cores[dst]
+        assert topo.may_write(core, d)
+        rid, pid, _ = topo.addr(d)
+        if wait is not None:
+            g.wait_ge(S[wait], arrive.get(wait, 1))
+        ov, iv = T[o[0]][:, o[1]:o[2]], T[i[0]][:, i[1]:i[2]]
+        if codes:
+            ov, iv = ov.bitcast(u8), iv.bitcast(u8)
+        g.remote_dma(ov, iv, S[sem], S.sent, pid, rid, m)
+        total += _count(m)
     g.wait_ge(S.sent, total)
     if last:
-        g.wait_ge(S.st, 16 * stores)
+        g.wait_ge(S.st, 32)

from concourse.mybir import dt, AluOpType, ActivationFunctionType

N, MB, G, NC = 10, 3, 2, 128
C = 0.019
NG = 2
GW = MB * NC // NG
TW = 4 * GW
WW = G * NC
SINGLE = 0
PAIRS = [(r, r + 1) for r in range(1, N - 1, 2)]

SCRATCH = {
    "wt": ("sbuf", [128, G * 4 * NC], "bfloat16"),
    "wq": ("sbuf", [128, WW], "float8_e4m3fn_x4"),
    "wp": ("sbuf", [128, WW], "uint8"),
    "fq": ("sbuf", [128, WW], "float8_e4m3fn_x4"),
    "fp": ("sbuf", [128, WW], "uint8"),
    "rp": ("sbuf", [128, WW], "uint8"),
    "op": ("sbuf", [128, NG * GW], "uint8"),
    "ap": ("sbuf", [128, NG * GW], "uint8"),
    "ps": ("psum", [128, 512 * G * NG], "float32"),
    "ysb": ("sbuf", [128, G * NG * GW], "float32"),
}
SEMAPHORES = ["lw", "wqd", "warr", "rarr", "sent", "st"]
for _k in range(NG):
    SCRATCH["xt%d" % _k] = ("sbuf", [128, TW], "bfloat16")
    SCRATCH["h%d" % _k] = ("sbuf", [128, TW], "bfloat16")
    SCRATCH["oq%d" % _k] = ("sbuf", [128, GW], "float8_e4m3fn_x4")
    SCRATCH["aq%d" % _k] = ("sbuf", [128, GW], "float8_e4m3fn_x4")
    SEMAPHORES += ["lx%d" % _k, "arr%d" % _k, "hd%d" % _k, "qd%d" % _k]
    SEMAPHORES += ["z%d%d" % (_k, _i) for _i in range(G)] + ["c%d%d" % (_k, _i) for _i in range(G)]


def _count(mask):
    return bin(mask).count("1")


def _layout(T, topo):
    cores = T.cores

    def chip(r):
        return topo.chip(cores[r])

    def mask(a, b):
        return topo.mask(cores[a], cores[b])

    ways = [[SINGLE], [SINGLE]]
    for a, b in PAIRS:
        keep = int(chip(ways[0][-1]) == chip(a)) + int(chip(ways[1][-1]) == chip(b))
        turn = int(chip(ways[0][-1]) == chip(b)) + int(chip(ways[1][-1]) == chip(a))
        u, v = (a, b) if keep >= turn else (b, a)
        ways[0].append(u)
        ways[1].append(v)
    for w in ways:
        w.append(N - 1)
    ways.sort(key=lambda w: sum(int(chip(w[j]) == chip(w[j + 1])) for j in range(len(w) - 1)))

    near = None
    for a, b in PAIRS:
        for u in (a, b):
            if chip(u) == chip(SINGLE):
                near = u

    out = []

    def tile(src, k, dst, slot, m):
        out.append((src, "qd%d" % k, dst, ("aq%d" % slot, 0, GW), ("oq%d" % k, 0, GW), True, "arr%d" % slot, m))
        out.append((src, None, dst, ("ap", GW * slot, GW * slot + GW), ("op", GW * k, GW * k + GW), False, "arr%d" % slot, m))

    m = mask(N - 1, SINGLE)
    out.append((N - 1, "qd0", SINGLE, ("aq0", 0, GW), ("oq0", 0, GW), True, "arr0", m))
    out.append((N - 1, "qd1", SINGLE, ("ap", 0, NG * GW), ("op", 0, NG * GW), False, "arr0", m))
    out.append((N - 1, None, SINGLE, ("aq1", 0, GW), ("oq1", 0, GW), True, "arr1", m))

    hop = {}
    for w in ways:
        for j in range(1, len(w) - 1):
            hop[w[j]] = w[j + 1]
    passed = []
    for a, b in PAIRS:
        for u, v in ((a, b), (b, a)):
            m = mask(u, v)
            via = [SINGLE if v == near else None, hop[u] if chip(hop[u]) == chip(u) else None]
            seq = []
            for i in range(G):
                if via[i] is not None:
                    lo, hi = NC * i, NC * i + NC
                    seq.append((via[i], ("rp", lo, hi), ("wp", lo, hi), False, "rarr", mask(u, via[i])))
                    passed.append((via[i], "rarr", v, ("fp", lo, hi), ("rp", lo, hi), False, "warr", mask(via[i], v)))
            seq.append((v, ("fq", 0, WW), ("wq", 0, WW), True, "warr", m))
            if via == [None] * G:
                seq.append((v, ("fp", 0, WW), ("wp", 0, WW), False, "warr", m))
            else:
                for i in range(G):
                    if via[i] is None:
                        seq.append((v, ("fp", NC * i, NC * i + NC), ("wp", NC * i, NC * i + NC), False, "warr", m))
            for n, t in enumerate(seq):
                out.append((u, "wqd" if n == 0 else None) + t)
    out += passed

    for q, w in enumerate(ways):
        m = mask(SINGLE, w[1])
        spare = m & ~mask(SINGLE, ways[1 - q][1])
        tile(SINGLE, q, w[1], 0, spare if spare else m)
        for j in range(1, len(w) - 1):
            tile(w[j], 1, w[j + 1], q if w[j + 1] == N - 1 else 0, mask(w[j], w[j + 1]))
    return out


def _pieces(q, i):
    out, j = [], 0
    while j < GW:
        m, o = divmod(GW * q + j, NC)
        w = min(NC - o, GW - j)
        out.append((j, NC * (G * m + i) + o, w))
        j += w
    return out


def rank_program(g, core, T, topo):
    rank = T.rank_of(core)
    if rank is None:
        return
    last = rank == N - 1
    pair = None
    for p in PAIRS:
        if rank in p:
            pair = p
    paired = pair is not None
    S, V, A, PE, SY = T.sem, g.vector, g.scalar, g.tensor, g.sync
    u8 = dt.uint8

    def bank(k, i, lo=0, hi=GW):
        b = 512 * (G * k + i)
        return T.ps[:, b + lo:b + hi]

    writes = _layout(T, topo)
    arrive = {}
    for _, _, dst, _, _, _, sem, m in writes:
        if dst == rank:
            arrive[sem] = arrive.get(sem, 0) + _count(m)

    if last:
        SY.dma_start(T.xt0[:], T.x[:, 0:TW]).then_inc(S.lx0, 16)
        SY.dma_start(T.xt1[:], T.x[:, TW:2 * TW]).then_inc(S.lx1, 16)
        SY.dma_start(T.wt[:], T.w[:]).then_inc(S.lw, 16)
        for q in range(NG):
            V.wait_ge(S["lx%d" % q], 16)
            V.quantize_mx(T["oq%d" % q][:], T.op[:, GW * q:GW * q + GW], T["xt%d" % q][:]).then_inc(S["qd%d" % q], 1)
    else:
        SY.dma_start(T.wt[:], T.w[:]).then_inc(S.lw, 16)
    V.wait_ge(S.lw, 16)
    V.quantize_mx(T.wq[:], T.wp[:], T.wt[:]).then_inc(S.wqd, 1)

    for k in range(NG):
        own = not paired or pair[k] == rank
        wq, wp = (T.wq, T.wp) if own else (T.fq, T.fp)
        if own:
            PE.wait_ge(S.wqd, 1)
        else:
            PE.wait_ge(S.warr, arrive["warr"])
        if paired and k == 1:
            mq, mp = T.oq0[:], T.op[:, 0:GW]
            PE.wait_ge(S.qd0, 1)
        else:
            mq, mp = T["aq%d" % k][:], T.ap[:, GW * k:GW * k + GW]
            PE.wait_ge(S["arr%d" % k], arrive["arr%d" % k])
        for i in range(G):
            PE.matmul_mx(bank(k, i), wq[:, NC * i:NC * i + NC], wp[:, NC * i:NC * i + NC],
                         mq, mp, True, True).then_inc(S["z%d%d" % (k, i)], 1)

    for k in range(NG):
        z0, z1 = S["z%d0" % k], S["z%d1" % k]
        if last:
            A.wait_ge(z0, 1)
            for j, yc, w in _pieces(k, 0):
                A.activation(T.ysb[:, yc:yc + w], bank(k, 0, j, j + w), ActivationFunctionType.Copy).then_inc(S["c%d0" % k], 1)
            V.wait_ge(z1, 1)
            for j, yc, w in _pieces(k, 1):
                V.tensor_copy(T.ysb[:, yc:yc + w], bank(k, 1, j, j + w)).then_inc(S["c%d1" % k], 1)
        else:
            h, hd = T["h%d" % k], S["hd%d" % k]
            A.wait_ge(z0, 1)
            A.activation(h[:, 0:TW:4], bank(k, 0), ActivationFunctionType.Relu, scale=C).then_inc(hd, 1)
            A.activation(h[:, 1:TW:4], bank(k, 0), ActivationFunctionType.Relu, scale=-C).then_inc(hd, 1)
            V.wait_ge(z1, 1)
            V.tensor_scalar(h[:, 2:TW:4], bank(k, 1), 0.0, C, AluOpType.max, AluOpType.mult).then_inc(hd, 1)
            V.tensor_scalar(h[:, 3:TW:4], bank(k, 1), -C, 0.0, AluOpType.mult, AluOpType.max).then_inc(hd, 1)
            V.wait_ge(hd, 4)
            V.quantize_mx(T["oq%d" % k][:], T.op[:, GW * k:GW * k + GW], h[:]).then_inc(S["qd%d" % k], 1)
    if last:
        cut, grown = 0, True
        while grown:
            grown = False
            for i in range(G):
                for _, yc, w in _pieces(0, i):
                    if yc == cut:
                        cut, grown = cut + w, True
        for i in range(G):
            SY.wait_ge(S["c0%d" % i], len(_pieces(0, i)))
        SY.dma_start(T.y[:, 0:cut], T.ysb[:, 0:cut]).then_inc(S.st, 16)
        for i in range(G):
            SY.wait_ge(S["c1%d" % i], len(_pieces(1, i)))
        SY.dma_start(T.y[:, cut:], T.ysb[:, cut:]).then_inc(S.st, 16)

    total = 0
    for src, wait, dst, o, i, codes, sem, m in writes:
        if src != rank:
            continue
        d = T.cores[dst]
        assert topo.may_write(core, d)
        rid, pid, _ = topo.addr(d)
        if wait is not None:
            g.wait_ge(S[wait], arrive.get(wait, 1))
        ov, iv = T[o[0]][:, o[1]:o[2]], T[i[0]][:, i[1]:i[2]]
        if codes:
            ov, iv = ov.bitcast(u8), iv.bitcast(u8)
        g.remote_dma(ov, iv, S[sem], S.sent, pid, rid, m)
        total += _count(m)
    g.wait_ge(S.sent, total)
    if last:
        g.wait_ge(S.st, 32)
